import numpy as np, ml_dtypes
CORES = [24,25,26,27,28,29,30,31]
N = 8
import mx_ref
BF = ml_dtypes.bfloat16
def cols(t, e):
    v = np.concatenate([t.reshape(128, -1, 4), np.zeros((128, 1, 4), BF)], axis=1)
    return np.ascontiguousarray(v[:, e]).reshape(128, -1)
def f(rng, *shape):
    return mx_ref.flush((rng.standard_normal(shape, dtype=np.float32) * np.exp2(rng.integers(-2, 3, shape[:-1] + (1,)))).astype(BF))
def wide(rng, *shape, cols=0):
    v = rng.standard_normal(shape, dtype=np.float32) * np.exp2(rng.integers(-12, 13, shape)).astype(np.float32)
    if cols: v *= np.repeat(np.exp2(rng.integers(-cols, cols + 1, shape[:-2] + (1, shape[-1] // 4))) * (rng.random(shape[:-2] + (1, shape[-1] // 4)) > 0.0625), 4, axis=-1).astype(np.float32)
    return mx_ref.flush(v.astype(BF))
T, NBIT, K, O = 192, 8, 256, 2
def planes(rng):
    v = np.zeros((N, 128, 512), BF); v[:, :, :4 * NBIT] = f(rng, N, 128, 4 * NBIT); return v
def setup_inputs(rng):
    return {"x": f(rng, N, 128, 4 * T), "hp": planes(rng), "e": f(rng, N, 128, 4 * K), "qw": f(rng, N, 128, O * 512)}
def setup_inputs_zero(rng):
    d = setup_inputs(rng)
    for r in rng.permutation(N)[:N // 2]:
        i = rng.integers(0, NBIT); d["hp"][r, :, 4 * i:4 * i + 4] = 0
    for r in range(N):
        for j in rng.permutation(T)[:T // 8]: d["x"][r, :, 4 * j:4 * j + 4] = 0
    return d
def setup_inputs_onebucket(rng):
    d = setup_inputs(rng); d["x"] = np.tile(d["hp"][rng.integers(0, N)][:, :4], (N, 1, T)); return d
def setup_inputs_all(rng):
    d = setup_inputs(rng); g = f(rng, 128, 4).astype(np.float32)[None, :, None, :]
    d["hp"][:, :, :4 * NBIT] = (g * np.exp2(rng.integers(0, 4, (N, 1, NBIT, 1)))).reshape(N, 128, -1).astype(BF)
    s = np.stack([rng.permutation(T) % 2 * 2 - 1 for r in range(N)]) * np.exp2(rng.integers(0, 4, (N, T)))
    d["x"] = (g * s[:, None, :, None]).reshape(N, 128, -1).astype(BF); return d
def setup_inputs_small(rng):
    d = setup_inputs(rng)
    for k in ("x", "hp"):
        v = d[k].astype(np.float32) * np.float32(2.0 ** -24)
        d[k] = mx_ref.flush(np.where(np.abs(v) < np.float32(2.0 ** -30), np.float32(0), v).astype(BF))
    return d
def setup_inputs_spread(rng):
    d = setup_inputs(rng); d["x"] = wide(rng, N, 128, 4 * T, cols=8); d["e"] = wide(rng, N, 128, 4 * K, cols=8); return d
def check_inputs(d):
    b = []
    if (np.asarray(d["hp"]).astype(np.float32)[:, :, 4 * NBIT:] != 0).any(): b.append("hp")
    return b
def reference(x, hp, e, qw):
    X = [mx_ref.quantize(x[r]) for r in range(N)]
    H = [mx_ref.quantize(hp[q]) for q in range(N)]
    W = [[mx_ref.quantize(np.ascontiguousarray(qw[r][:, 512 * o:512 * o + 512])) for o in range(O)] for r in range(N)]
    y = np.zeros((N, 128, N * O * T), np.float32); bk = np.zeros((N, N, T), np.float32)
    for r in range(N):
        for q in range(N):
            s = mx_ref.matmul(H[q], X[r])
            b = np.zeros(T, int)
            for i in range(NBIT): b += 2 ** i * (s[i] > 0)
            bk[r, q] = b
            c = mx_ref.quantize(cols(e[q], b))
            for o in range(O):
                k = (q * O + o) * T
                y[r][:, k:k + T] = mx_ref.matmul(W[r][o], c)
    return {"y": y, "bk": bk}

@@ -1,0 +1,193 @@
+from concourse.bass import DstId, RemoteDMATransfer
+from concourse.mybir import dt, AluOpType, ActivationFunctionType
+
+N, TOK, NBIT, K, O = 8, 192, 8, 256, 2
+RUNS = TOK // 16
+PL = N * NBIT
+OWN = PL
+
+SCRATCH = {
+    "hpt": ("sbuf", [128, 512], "bfloat16"),
+    "et": ("sbuf", [128, 4 * K], "bfloat16"),
+    "xt": ("sbuf", [128, RUNS, 64], "bfloat16"),
+    "x8": ("sbuf", [128, RUNS, 512], "bfloat16"),
+    "qwt": ("sbuf", [128, O * 512], "bfloat16"),
+    "hpc": ("sbuf", [128, OWN + 128], "float8_e4m3fn_x4"),
+    "hps": ("sbuf", [128, OWN + 128], "uint8"),
+    "ec": ("sbuf", [128, N * K], "float8_e4m3fn_x4"),
+    "es": ("sbuf", [128, N * K], "uint8"),
+    "xc": ("sbuf", [128, RUNS * 128], "float8_e4m3fn_x4"),
+    "xs": ("sbuf", [128, RUNS * 128], "uint8"),
+    "wc": ("sbuf", [128, O * 128], "float8_e4m3fn_x4"),
+    "ws": ("sbuf", [128, O * 128], "uint8"),
+    "half": ("sbuf", [128, RUNS * PL], "bfloat16"),
+    "bits": ("sbuf", [128, RUNS * PL], "bfloat16"),
+    "scan": ("sbuf", [128, RUNS * PL], "bfloat16"),
+    "buck": ("sbuf", [128, N * RUNS], "float32"),
+    "offs": ("sbuf", [128, N * RUNS], "uint16"),
+    "bkt": ("sbuf", [128, 32], "float32"),
+    "tab0": ("sbuf", [128, N * K], "float32"),
+    "tab1": ("sbuf", [128, N * K], "float32"),
+    "yb": ("sbuf", [128, N * O * TOK], "float32"),
+    "acc": ("psum", [128, 4096], "float32"),
+}
+SEMAPHORES = (["hpl", "el", "xl", "qwl", "zero", "halfm", "qh", "qe", "xv", "xa", "qx", "qq", "bm", "cmp", "scn", "rord",
+               "lst", "tm0", "tm1", "tc0", "tc1", "bkr", "stored", "sent", "hpa"]
+              + ["ea%d" % q for q in range(N)] + ["yr%d" % q for q in range(N)])
+
+VCOPY = 5
+
+
+def rank_program(g, core, T, topo):
+    rank = T.rank_of(core)
+    if rank is None:
+        return
+    S = T.sem
+    v, a, t, sy = g.vector, g.scalar, g.tensor, g.sync
+    Copy = ActivationFunctionType.Copy
+    cores = T.cores
+    peers = sorted((q for q in range(N) if q != rank), key=lambda q: (topo.die(cores[q]) != topo.die(core), q ^ rank))
+    near = [q for q in peers if topo.die(cores[q]) == topo.die(core)]
+    far = [q for q in peers if q not in near]
+    groups = [near] + [far[i:i + 2] for i in range(0, len(far), 2)]
+    groups = [m for m in groups if m]
+    pairs = []
+    for q in [rank] + peers:
+        if q // 2 not in pairs:
+            pairs.append(q // 2)
+
+    def slot(q):
+        return slot_at(rank, q)
+
+    def slot_at(r, q):
+        return (q ^ r) - 1 if q != r else N - 1
+
+    def send(dsts, src, views, sem):
+        g.remote_dma_fused([RemoteDMATransfer(
+            dst_ids=[DstId(rid=topo.addr(cores[q])[0], pnc=topo.addr(cores[q])[1]) for q in dsts],
+            dma_engine_mask=topo.mask(core, cores[dsts[0]]), remote_sem=sem, srcs=[src], dsts=views)],
+            local_sem=S.sent)
+
+    sy.dma_start(T.hpt[:, 0:4 * NBIT], T.hp[:, 0:4 * NBIT]).then_inc(S.hpl, 16)
+    a.dma_start(T.et[:], T.e[:]).then_inc(S.el, 16)
+    sy.dma_start(T.xt[:], T.x[:]).then_inc(S.xl, 16)
+    a.dma_start(T.qwt[:], T.qw[:]).then_inc(S.qwl, 16)
+
+    g.wait_ge(S.qh, 1)
+    c0 = [8 + NBIT * slot_at(q, rank) for q in peers]
+    send(peers, T.hpc[:, OWN:OWN + NBIT].bitcast(dt.uint8),
+         [T.hpc[:, k:k + NBIT].bitcast(dt.uint8) for k in c0], S.hpa)
+    send(peers, T.hps[:, OWN:OWN + NBIT], [T.hps[:, k:k + NBIT] for k in c0], S.hpa)
+    g.wait_ge(S.qe, 1)
+    mine = slice(K * rank, K * rank + K)
+    ncalls = 2
+    for m in groups:
+        send(m, T.ec[:, mine].bitcast(dt.uint8), [T.ec[:, mine].bitcast(dt.uint8) for q in m], S["ea%d" % rank])
+        send(m, T.es[:, mine], [T.es[:, mine] for q in m], S["ea%d" % rank])
+        ncalls += 2
+    neng = len(topo.engines(core, cores[peers[0]]))
+    g.wait_ge(S.sent, ncalls * neng)
+
+    v.memset(T.hpt[:, 4 * NBIT:512], 0.0).then_inc(S.zero, 1)
+    v.memset(T.half[:], 0.5).then_inc(S.halfm, 1)
+    v.wait_ge(S.halfm, 1)
+    v.memset(T.half[:, 0:RUNS * PL:NBIT], 0.0).then_inc(S.halfm, 1)
+    v.wait_ge(S.zero, 1)
+    v.wait_ge(S.hpl, 16)
+    v.quantize_mx(T.hpc[:, OWN:OWN + 128], T.hps[:, OWN:OWN + 128], T.hpt[:]).then_inc(S.qh, 1)
+    v.wait_ge(S.el, 16)
+    v.quantize_mx(T.ec[:, mine], T.es[:, mine], T.et[:]).then_inc(S.qe, 1)
+    v.wait_ge(S.xl, 16)
+    a.wait_ge(S.xl, 16)
+    for h in range(0, RUNS, 4):
+        for k in range(8):
+            o_, i_ = T.x8[:, h:h + 4, 64 * k:64 * k + 64], T.xt[:, h:h + 4, :]
+            if k < VCOPY:
+                v.tensor_copy(o_, i_).then_inc(S.xv, 1)
+            else:
+                a.activation(o_, i_, Copy).then_inc(S.xa, 1)
+        v.wait_ge(S.xv, (h // 4 + 1) * VCOPY)
+        v.wait_ge(S.xa, (h // 4 + 1) * (8 - VCOPY))
+        for c in range(h, h + 4):
+            v.quantize_mx(T.xc[:, 128 * c:128 * c + 128], T.xs[:, 128 * c:128 * c + 128], T.x8[:, c, :]).then_inc(S.qx, 1)
+    v.wait_ge(S.qwl, 16)
+    v.quantize_mx(T.wc[:], T.ws[:], T.qwt[:]).then_inc(S.qq, 1)
+
+    t.wait_ge(S.qh, 1)
+    t.wait_ge(S.hpa, (N - 1) * 2 * neng)
+    for c in range(RUNS):
+        t.wait_ge(S.qx, c + 1)
+        if c >= 8:
+            t.wait_ge(S.cmp, c - 7)
+        b = 512 * (c % 8)
+        t.matmul_mx(T.acc[:, b:b + 128], T.xc[:, 128 * c:128 * c + 128], T.xs[:, 128 * c:128 * c + 128],
+                    T.hpc[:, 8:136], T.hps[:, 8:136], True, True).then_inc(S.bm, 1)
+    t.wait_ge(S.qq, 1)
+    t.wait_ge(S.qe, 1)
+    bank = {}
+    for i, u in enumerate(pairs):
+        for q in (2 * u, 2 * u + 1):
+            if q != rank:
+                t.wait_ge(S["ea%d" % q], 2 * neng)
+        for o in range(O):
+            b = (4 + 2 * i + o) % 8
+            bank[i, o] = 512 * b
+            t.wait_ge(S.cmp, b + 1 if b >= 4 else b + 9)
+            t.matmul_mx(T.acc[:, 512 * b:512 * b + 512], T.wc[:, 128 * o:128 * o + 128], T.ws[:, 128 * o:128 * o + 128],
+                        T.ec[:, 512 * u:512 * u + 512], T.es[:, 512 * u:512 * u + 512], True, True
+                        ).then_inc(S["tm%d" % o], 1)
+
+    for c in range(RUNS):
+        v.wait_ge(S.bm, c + 1)
+        b = 512 * (c % 8)
+        v.tensor_scalar(T.bits[:, PL * c:PL * c + PL], T.acc[:, b:b + PL], 0.0, 128.0, AluOpType.is_gt, AluOpType.mult
+                        ).then_inc(S.cmp, 1)
+    v.wait_ge(S.cmp, RUNS)
+    v.wait_ge(S.halfm, 2)
+    v.tensor_tensor_scan(T.scan[:], T.half[:], T.bits[:], 0.0, AluOpType.mult, AluOpType.add).then_inc(S.scn, 1)
+
+    a.wait_ge(S.scn, 1)
+    v.wait_ge(S.scn, 1)
+    for q in range(N):
+        i_ = T.scan[:, NBIT * slot(q) + NBIT - 1:RUNS * PL:PL]
+        o_ = T.buck[:, RUNS * q:RUNS * q + RUNS]
+        if q % 2 == 0:
+            v.tensor_copy(o_, i_).then_inc(S.rord, 1)
+        else:
+            a.activation(o_, i_, Copy).then_inc(S.rord, 1)
+    v.wait_ge(S.rord, N)
+    v.tensor_copy(T.offs[:], T.buck[:]).then_inc(S.lst, 1)
+    v.wait_ge(S.lst, 1)
+
+    for i, u in enumerate(pairs):
+        for o, eng in ((0, v), (1, a)):
+            w = slice(512 * u, 512 * u + 512)
+            tab, tc = T["tab%d" % o], S["tc%d" % o]
+            eng.wait_ge(S["tm%d" % o], i + 1)
+            if o == 0:
+                v.tensor_copy(tab[:, w], T.acc[:, bank[i, o]:bank[i, o] + 512]).then_inc(tc, 1)
+            else:
+                a.activation(tab[:, w], T.acc[:, bank[i, o]:bank[i, o] + 512], Copy).then_inc(tc, 1)
+                if i == 0:
+                    a.wait_ge(S.lst, 1)
+            eng.wait_ge(tc, i + 1)
+            for q in (2 * u, 2 * u + 1):
+                k = (q * O + o) * TOK
+                pick = tab[:, K * q:K * q + K].indirect(T.offs[:, RUNS * q:RUNS * q + RUNS])
+                if o == 0:
+                    v.tensor_copy(T.yb[:, k:k + TOK], pick).then_inc(S["yr%d" % q], 1)
+                else:
+                    a.activation(T.yb[:, k:k + TOK], pick, Copy).then_inc(S["yr%d" % q], 1)
+        if i == 0:
+            for b in range(0, N * RUNS, 32):
+                v.transpose(T.bkt[b:b + 32, :], T.buck[b:b + 32, b:b + 32]).then_inc(S.bkr, 1)
+
+    for i, u in enumerate(pairs):
+        for q in (2 * u, 2 * u + 1):
+            sy.wait_ge(S["yr%d" % q], O)
+        w = slice(2 * O * TOK * u, 2 * O * TOK * (u + 1))
+        sy.dma_start(T.y[:, w], T.yb[:, w]).then_inc(S.stored, 16)
+        if i == 0:
+            sy.wait_ge(S.bkr, N * RUNS // 32)
+            sy.dma_start(T.bk[:], T.bkt[0:N * RUNS, 0:16]).then_inc(S.stored, 16)
+    sy.wait_ge(S.stored, 16 * (len(pairs) + 1))

@@ -3,36 +3,41 @@ from concourse.mybir import dt, AluOpType, ActivationFunctionType
 
 N, TOK, NBIT, K, O = 8, 192, 8, 256, 2
 RUNS = TOK // 16
+X2 = 2 * TOK
 PL = N * NBIT
 OWN = PL
+H = N // 2
+HR = H * RUNS
 
 SCRATCH = {
     "hpt": ("sbuf", [128, 512], "bfloat16"),
     "et": ("sbuf", [128, 4 * K], "bfloat16"),
-    "xt": ("sbuf", [128, RUNS, 64], "bfloat16"),
-    "x8": ("sbuf", [128, RUNS, 512], "bfloat16"),
+    "xt": ("sbuf", [128, 3, 256], "bfloat16"),
+    "x2": ("sbuf", [128, 3, 512], "bfloat16"),
     "qwt": ("sbuf", [128, O * 512], "bfloat16"),
     "hpc": ("sbuf", [128, OWN + 128], "float8_e4m3fn_x4"),
     "hps": ("sbuf", [128, OWN + 128], "uint8"),
     "ec": ("sbuf", [128, N * K], "float8_e4m3fn_x4"),
     "es": ("sbuf", [128, N * K], "uint8"),
-    "xc": ("sbuf", [128, RUNS * 128], "float8_e4m3fn_x4"),
-    "xs": ("sbuf", [128, RUNS * 128], "uint8"),
+    "xc": ("sbuf", [128, X2], "float8_e4m3fn_x4"),
+    "xs": ("sbuf", [128, X2], "uint8"),
     "wc": ("sbuf", [128, O * 128], "float8_e4m3fn_x4"),
     "ws": ("sbuf", [128, O * 128], "uint8"),
-    "half": ("sbuf", [128, RUNS * PL], "bfloat16"),
-    "bits": ("sbuf", [128, RUNS * PL], "bfloat16"),
-    "scan": ("sbuf", [128, RUNS * PL], "bfloat16"),
-    "buck": ("sbuf", [128, N * RUNS], "float32"),
+    "half": ("sbuf", [128, X2], "bfloat16"),
+    "bits": ("sbuf", [128, X2], "bfloat16"),
+    "turn": ("sbuf", [128, X2], "bfloat16"),
+    "scan": ("sbuf", [128, X2], "bfloat16"),
+    "buck": ("sbuf", [128, HR], "float32"),
     "offs": ("sbuf", [128, N * RUNS], "uint16"),
-    "bkt": ("sbuf", [128, 32], "float32"),
+    "bkp": ("sbuf", [128, 64], "float32"),
+    "bkt": ("sbuf", [128, 64], "float32"),
     "tab0": ("sbuf", [128, N * K], "float32"),
     "tab1": ("sbuf", [128, N * K], "float32"),
     "yb": ("sbuf", [128, N * O * TOK], "float32"),
     "acc": ("psum", [128, 4096], "float32"),
 }
-SEMAPHORES = (["hpl", "el", "xl", "qwl", "zero", "halfm", "qh", "qe", "xv", "xa", "qx", "qq", "bm", "cmp", "scn", "rord",
-               "lst", "tm0", "tm1", "tc0", "tc1", "bkr", "stored", "sent", "hpa"]
+SEMAPHORES = (["hpl", "el", "xl", "qwl", "zero", "halfm", "qh", "qe", "xv", "xa", "qx", "qq", "bm", "cmp", "trn", "scn",
+               "rord", "lst", "tm0", "tm1", "tco", "tc0", "tc1", "bkc", "bkr", "stored", "sent", "hpa"]
               + ["ea%d" % q for q in range(N)] + ["yr%d" % q for q in range(N)])
 
 VCOPY = 5
@@ -55,12 +60,10 @@ def rank_program(g, core, T, topo):
     for q in [rank] + peers:
         if q // 2 not in pairs:
             pairs.append(q // 2)
-
-    def slot(q):
-        return slot_at(rank, q)
+    units = [[rank], [rank ^ 1]] + [[2 * u, 2 * u + 1] for u in pairs[1:]]
 
     def slot_at(r, q):
-        return (q ^ r) - 1 if q != r else N - 1
+        return H * int(q // H == r // H) + ((q % H) ^ (r % H) ^ (H - 1))
 
     def send(dsts, src, views, sem):
         g.remote_dma_fused([RemoteDMATransfer(
@@ -90,8 +93,9 @@ def rank_program(g, core, T, topo):
 
     v.memset(T.hpt[:, 4 * NBIT:512], 0.0).then_inc(S.zero, 1)
     v.memset(T.half[:], 0.5).then_inc(S.halfm, 1)
+    v.memset(T.bkp[:], 0.0).then_inc(S.bkc, 1)
     v.wait_ge(S.halfm, 1)
-    v.memset(T.half[:, 0:RUNS * PL:NBIT], 0.0).then_inc(S.halfm, 1)
+    v.memset(T.half[:, 0:X2:NBIT], 0.0).then_inc(S.halfm, 1)
     v.wait_ge(S.zero, 1)
     v.wait_ge(S.hpl, 16)
     v.quantize_mx(T.hpc[:, OWN:OWN + 128], T.hps[:, OWN:OWN + 128], T.hpt[:]).then_inc(S.qh, 1)
@@ -99,79 +103,84 @@ def rank_program(g, core, T, topo):
     v.quantize_mx(T.ec[:, mine], T.es[:, mine], T.et[:]).then_inc(S.qe, 1)
     v.wait_ge(S.xl, 16)
     a.wait_ge(S.xl, 16)
-    for h in range(0, RUNS, 4):
-        for k in range(8):
-            o_, i_ = T.x8[:, h:h + 4, 64 * k:64 * k + 64], T.xt[:, h:h + 4, :]
-            if k < VCOPY:
-                v.tensor_copy(o_, i_).then_inc(S.xv, 1)
-            else:
-                a.activation(o_, i_, Copy).then_inc(S.xa, 1)
-        v.wait_ge(S.xv, (h // 4 + 1) * VCOPY)
-        v.wait_ge(S.xa, (h // 4 + 1) * (8 - VCOPY))
-        for c in range(h, h + 4):
-            v.quantize_mx(T.xc[:, 128 * c:128 * c + 128], T.xs[:, 128 * c:128 * c + 128], T.x8[:, c, :]).then_inc(S.qx, 1)
+    for n in range(8):
+        j, k = n // 2, n % 2
+        o_, i_ = T.x2[:, :, 128 * j + 64 * k:128 * j + 64 * k + 64], T.xt[:, :, 64 * j:64 * j + 64]
+        if n < VCOPY:
+            v.tensor_copy(o_, i_).then_inc(S.xv, 1)
+        else:
+            a.activation(o_, i_, Copy).then_inc(S.xa, 1)
+    v.wait_ge(S.xv, VCOPY)
+    v.wait_ge(S.xa, 8 - VCOPY)
+    for c in range(3):
+        v.quantize_mx(T.xc[:, 128 * c:128 * c + 128], T.xs[:, 128 * c:128 * c + 128], T.x2[:, c, :]).then_inc(S.qx, 1)
     v.wait_ge(S.qwl, 16)
     v.quantize_mx(T.wc[:], T.ws[:], T.qwt[:]).then_inc(S.qq, 1)
 
     t.wait_ge(S.qh, 1)
+    t.wait_ge(S.qx, 3)
     t.wait_ge(S.hpa, (N - 1) * 2 * neng)
-    for c in range(RUNS):
-        t.wait_ge(S.qx, c + 1)
-        if c >= 8:
-            t.wait_ge(S.cmp, c - 7)
-        b = 512 * (c % 8)
-        t.matmul_mx(T.acc[:, b:b + 128], T.xc[:, 128 * c:128 * c + 128], T.xs[:, 128 * c:128 * c + 128],
-                    T.hpc[:, 8:136], T.hps[:, 8:136], True, True).then_inc(S.bm, 1)
+    t.matmul_mx(T.acc[:, 0:X2], T.hpc[:, 8:136], T.hps[:, 8:136], T.xc[:], T.xs[:], True, True).then_inc(S.bm, 1)
     t.wait_ge(S.qq, 1)
     t.wait_ge(S.qe, 1)
     bank = {}
-    for i, u in enumerate(pairs):
-        for q in (2 * u, 2 * u + 1):
+    for i, m in enumerate(units):
+        for q in m:
             if q != rank:
                 t.wait_ge(S["ea%d" % q], 2 * neng)
+        w = slice(K * m[0], K * m[0] + K * len(m))
         for o in range(O):
-            b = (4 + 2 * i + o) % 8
+            b = 1 + O * i + o
+            if b == 8:
+                t.wait_ge(S.cmp, 1)
+            if b > 8:
+                t.wait_ge(S.tco, O)
+            b = b % 8
             bank[i, o] = 512 * b
-            t.wait_ge(S.cmp, b + 1 if b >= 4 else b + 9)
-            t.matmul_mx(T.acc[:, 512 * b:512 * b + 512], T.wc[:, 128 * o:128 * o + 128], T.ws[:, 128 * o:128 * o + 128],
-                        T.ec[:, 512 * u:512 * u + 512], T.es[:, 512 * u:512 * u + 512], True, True
-                        ).then_inc(S["tm%d" % o], 1)
+            t.matmul_mx(T.acc[:, 512 * b:512 * b + K * len(m)], T.wc[:, 128 * o:128 * o + 128],
+                        T.ws[:, 128 * o:128 * o + 128], T.ec[:, w], T.es[:, w], True, True).then_inc(S["tm%d" % o], 1)
 
-    for c in range(RUNS):
-        v.wait_ge(S.bm, c + 1)
-        b = 512 * (c % 8)
-        v.tensor_scalar(T.bits[:, PL * c:PL * c + PL], T.acc[:, b:b + PL], 0.0, 128.0, AluOpType.is_gt, AluOpType.mult
-                        ).then_inc(S.cmp, 1)
-    v.wait_ge(S.cmp, RUNS)
+    v.wait_ge(S.bm, 1)
+    v.tensor_scalar(T.bits[0:PL, :], T.acc[0:PL, 0:X2], 0.0, 128.0, AluOpType.is_gt, AluOpType.mult).then_inc(S.cmp, 1)
+    v.wait_ge(S.cmp, 1)
+    v.transpose(T.turn[0:PL, :], T.bits[0:PL, :]).then_inc(S.trn, 1)
+    v.wait_ge(S.trn, 1)
     v.wait_ge(S.halfm, 2)
-    v.tensor_tensor_scan(T.scan[:], T.half[:], T.bits[:], 0.0, AluOpType.mult, AluOpType.add).then_inc(S.scn, 1)
-
-    a.wait_ge(S.scn, 1)
+    v.tensor_tensor_scan(T.scan[0:PL, :], T.half[0:PL, :], T.turn[0:PL, :], 0.0, AluOpType.mult, AluOpType.add
+                         ).then_inc(S.scn, 1)
     v.wait_ge(S.scn, 1)
-    for q in range(N):
-        i_ = T.scan[:, NBIT * slot(q) + NBIT - 1:RUNS * PL:PL]
-        o_ = T.buck[:, RUNS * q:RUNS * q + RUNS]
-        if q % 2 == 0:
-            v.tensor_copy(o_, i_).then_inc(S.rord, 1)
-        else:
-            a.activation(o_, i_, Copy).then_inc(S.rord, 1)
-    v.wait_ge(S.rord, N)
-    v.tensor_copy(T.offs[:], T.buck[:]).then_inc(S.lst, 1)
-    v.wait_ge(S.lst, 1)
+    for k in range(H):
+        low = (rank % H) ^ k ^ (H - 1)
+        v.tensor_copy(T.buck[0:PL, RUNS * low:RUNS * low + RUNS], T.scan[0:PL, NBIT * k + NBIT - 1:X2:NBIT * H]
+                      ).then_inc(S.rord, 1)
+    v.wait_ge(S.rord, H)
+    half_of = (1 - rank // H, rank // H)
+    for to in range(0, 128, 32):
+        for s in range(2):
+            h = HR * half_of[s]
+            v.tensor_copy(T.offs[to:to + 32, h:h + HR], T.buck[32 * s:32 * s + 32, :]).then_inc(S.lst, 1)
+    v.wait_ge(S.lst, 8)
 
-    for i, u in enumerate(pairs):
-        for o, eng in ((0, v), (1, a)):
-            w = slice(512 * u, 512 * u + 512)
+    for i, m in enumerate(units):
+        w = slice(K * m[0], K * m[0] + K * len(m))
+        for o, eng in ((1, a), (0, v)):
             tab, tc = T["tab%d" % o], S["tc%d" % o]
-            eng.wait_ge(S["tm%d" % o], i + 1)
-            if o == 0:
-                v.tensor_copy(tab[:, w], T.acc[:, bank[i, o]:bank[i, o] + 512]).then_inc(tc, 1)
+            b = slice(bank[i, o], bank[i, o] + K * len(m))
+            if i == 0:
+                if o == 1:
+                    for p in range(O):
+                        a.wait_ge(S["tm%d" % p], 1)
+                        a.activation(T["tab%d" % p][:, w], T.acc[:, bank[i, p]:bank[i, p] + K], Copy).then_inc(S.tco, 1)
+                    a.wait_ge(S.lst, 8)
+                eng.wait_ge(S.tco, O)
             else:
-                a.activation(tab[:, w], T.acc[:, bank[i, o]:bank[i, o] + 512], Copy).then_inc(tc, 1)
-                if i == 0:
-                    a.wait_ge(S.lst, 1)
-            eng.wait_ge(tc, i + 1)
-            for q in (2 * u, 2 * u + 1):
+                eng.wait_ge(S["tm%d" % o], i + 1)
+                if o == 0:
+                    v.tensor_copy(tab[:, w], T.acc[:, b]).then_inc(tc, 1)
+                else:
+                    a.activation(tab[:, w], T.acc[:, b], Copy).then_inc(tc, 1)
+                eng.wait_ge(tc, i)
+            for q in m:
                 k = (q * O + o) * TOK
                 pick = tab[:, K * q:K * q + K].indirect(T.offs[:, RUNS * q:RUNS * q + RUNS])
                 if o == 0:
@@ -179,15 +188,29 @@ def rank_program(g, core, T, topo):
                 else:
                     a.activation(T.yb[:, k:k + TOK], pick, Copy).then_inc(S["yr%d" % q], 1)
         if i == 0:
-            for b in range(0, N * RUNS, 32):
-                v.transpose(T.bkt[b:b + 32, :], T.buck[b:b + 32, b:b + 32]).then_inc(S.bkr, 1)
+            a.wait_ge(S.bkc, 1)
+            for j in range(2):
+                a.activation(T.bkp[0:PL, 32 * j:32 * j + 2 * RUNS], T.buck[0:PL, 2 * RUNS * j:2 * RUNS * j + 2 * RUNS],
+                             Copy).then_inc(S.bkc, 1)
+        if i == 1:
+            v.wait_ge(S.bkc, 3)
+            v.transpose(T.bkt[0:PL, :], T.bkp[0:PL, :]).then_inc(S.bkr, 1)
 
+    nst = 0
     for i, u in enumerate(pairs):
-        for q in (2 * u, 2 * u + 1):
-            sy.wait_ge(S["yr%d" % q], O)
-        w = slice(2 * O * TOK * u, 2 * O * TOK * (u + 1))
-        sy.dma_start(T.y[:, w], T.yb[:, w]).then_inc(S.stored, 16)
+        parts = [[2 * u], [2 * u + 1]] if i == len(pairs) - 1 else [[2 * u, 2 * u + 1]]
+        for m in parts:
+            for q in m:
+                sy.wait_ge(S["yr%d" % q], O)
+            w = slice(O * TOK * m[0], O * TOK * (m[0] + len(m)))
+            sy.dma_start(T.y[:, w], T.yb[:, w]).then_inc(S.stored, 16)
+            nst += 1
         if i == 0:
-            sy.wait_ge(S.bkr, N * RUNS // 32)
-            sy.dma_start(T.bk[:], T.bkt[0:N * RUNS, 0:16]).then_inc(S.stored, 16)
-    sy.wait_ge(S.stored, 16 * (len(pairs) + 1))
+            sy.wait_ge(S.bkr, 1)
+            for s in range(2):
+                for j in range(2):
+                    q = H * half_of[s] + 2 * j
+                    sy.dma_start(T.bk[q:q + 2, :], T.bkt[32 * s:32 * s + 2 * RUNS, 32 * j:32 * j + 16]
+                                 ).then_inc(S.stored, 16)
+                    nst += 1
+    sy.wait_ge(S.stored, 16 * nst)

from concourse.bass import DstId, RemoteDMATransfer
from concourse.mybir import dt, AluOpType, ActivationFunctionType

N, TOK, NBIT, K, O = 8, 192, 8, 256, 2
RUNS = TOK // 16
X2 = 2 * TOK
PL = N * NBIT
OWN = PL
H = N // 2
HR = H * RUNS

SCRATCH = {
    "hpt": ("sbuf", [128, 512], "bfloat16"),
    "et": ("sbuf", [128, 4 * K], "bfloat16"),
    "xt": ("sbuf", [128, 3, 256], "bfloat16"),
    "x2": ("sbuf", [128, 3, 512], "bfloat16"),
    "qwt": ("sbuf", [128, O * 512], "bfloat16"),
    "hpc": ("sbuf", [128, OWN + 128], "float8_e4m3fn_x4"),
    "hps": ("sbuf", [128, OWN + 128], "uint8"),
    "ec": ("sbuf", [128, N * K], "float8_e4m3fn_x4"),
    "es": ("sbuf", [128, N * K], "uint8"),
    "xc": ("sbuf", [128, X2], "float8_e4m3fn_x4"),
    "xs": ("sbuf", [128, X2], "uint8"),
    "wc": ("sbuf", [128, O * 128], "float8_e4m3fn_x4"),
    "ws": ("sbuf", [128, O * 128], "uint8"),
    "half": ("sbuf", [128, X2], "bfloat16"),
    "bits": ("sbuf", [128, X2], "bfloat16"),
    "turn": ("sbuf", [128, X2], "bfloat16"),
    "scan": ("sbuf", [128, X2], "bfloat16"),
    "buck": ("sbuf", [128, HR], "float32"),
    "offs": ("sbuf", [128, N * RUNS], "uint16"),
    "bkp": ("sbuf", [128, 64], "float32"),
    "bkt": ("sbuf", [128, 64], "float32"),
    "tab0": ("sbuf", [128, N * K], "float32"),
    "tab1": ("sbuf", [128, N * K], "float32"),
    "yb": ("sbuf", [128, N * O * TOK], "float32"),
    "acc": ("psum", [128, 4096], "float32"),
}
SEMAPHORES = (["hpl", "el", "xl", "qwl", "zero", "halfm", "qh", "qe", "xv", "xa", "qx", "qq", "bm", "cmp", "trn", "scn",
               "rord", "lst", "tm0", "tm1", "tco", "tc0", "tc1", "bkc", "bkr", "stored", "sent", "hpa"]
              + ["ea%d" % q for q in range(N)] + ["yr%d" % q for q in range(N)])

VCOPY = 5


def rank_program(g, core, T, topo):
    rank = T.rank_of(core)
    if rank is None:
        return
    S = T.sem
    v, a, t, sy = g.vector, g.scalar, g.tensor, g.sync
    Copy = ActivationFunctionType.Copy
    cores = T.cores
    peers = sorted((q for q in range(N) if q != rank), key=lambda q: (topo.die(cores[q]) != topo.die(core), q ^ rank))
    near = [q for q in peers if topo.die(cores[q]) == topo.die(core)]
    far = [q for q in peers if q not in near]
    groups = [near] + [far[i:i + 2] for i in range(0, len(far), 2)]
    groups = [m for m in groups if m]
    pairs = []
    for q in [rank] + peers:
        if q // 2 not in pairs:
            pairs.append(q // 2)
    units = [[rank], [rank ^ 1]] + [[2 * u, 2 * u + 1] for u in pairs[1:]]

    def slot_at(r, q):
        return H * int(q // H == r // H) + ((q % H) ^ (r % H) ^ (H - 1))

    def send(dsts, src, views, sem):
        g.remote_dma_fused([RemoteDMATransfer(
            dst_ids=[DstId(rid=topo.addr(cores[q])[0], pnc=topo.addr(cores[q])[1]) for q in dsts],
            dma_engine_mask=topo.mask(core, cores[dsts[0]]), remote_sem=sem, srcs=[src], dsts=views)],
            local_sem=S.sent)

    sy.dma_start(T.hpt[:, 0:4 * NBIT], T.hp[:, 0:4 * NBIT]).then_inc(S.hpl, 16)
    a.dma_start(T.et[:], T.e[:]).then_inc(S.el, 16)
    sy.dma_start(T.xt[:], T.x[:]).then_inc(S.xl, 16)
    a.dma_start(T.qwt[:], T.qw[:]).then_inc(S.qwl, 16)

    g.wait_ge(S.qh, 1)
    c0 = [8 + NBIT * slot_at(q, rank) for q in peers]
    send(peers, T.hpc[:, OWN:OWN + NBIT].bitcast(dt.uint8),
         [T.hpc[:, k:k + NBIT].bitcast(dt.uint8) for k in c0], S.hpa)
    send(peers, T.hps[:, OWN:OWN + NBIT], [T.hps[:, k:k + NBIT] for k in c0], S.hpa)
    g.wait_ge(S.qe, 1)
    mine = slice(K * rank, K * rank + K)
    ncalls = 2
    for m in groups:
        send(m, T.ec[:, mine].bitcast(dt.uint8), [T.ec[:, mine].bitcast(dt.uint8) for q in m], S["ea%d" % rank])
        send(m, T.es[:, mine], [T.es[:, mine] for q in m], S["ea%d" % rank])
        ncalls += 2
    neng = len(topo.engines(core, cores[peers[0]]))
    g.wait_ge(S.sent, ncalls * neng)

    v.memset(T.hpt[:, 4 * NBIT:512], 0.0).then_inc(S.zero, 1)
    v.memset(T.half[:], 0.5).then_inc(S.halfm, 1)
    v.memset(T.bkp[:], 0.0).then_inc(S.bkc, 1)
    v.wait_ge(S.halfm, 1)
    v.memset(T.half[:, 0:X2:NBIT], 0.0).then_inc(S.halfm, 1)
    v.wait_ge(S.zero, 1)
    v.wait_ge(S.hpl, 16)
    v.quantize_mx(T.hpc[:, OWN:OWN + 128], T.hps[:, OWN:OWN + 128], T.hpt[:]).then_inc(S.qh, 1)
    v.wait_ge(S.el, 16)
    v.quantize_mx(T.ec[:, mine], T.es[:, mine], T.et[:]).then_inc(S.qe, 1)
    v.wait_ge(S.xl, 16)
    a.wait_ge(S.xl, 16)
    for n in range(8):
        j, k = n // 2, n % 2
        o_, i_ = T.x2[:, :, 128 * j + 64 * k:128 * j + 64 * k + 64], T.xt[:, :, 64 * j:64 * j + 64]
        if n < VCOPY:
            v.tensor_copy(o_, i_).then_inc(S.xv, 1)
        else:
            a.activation(o_, i_, Copy).then_inc(S.xa, 1)
    v.wait_ge(S.xv, VCOPY)
    v.wait_ge(S.xa, 8 - VCOPY)
    for c in range(3):
        v.quantize_mx(T.xc[:, 128 * c:128 * c + 128], T.xs[:, 128 * c:128 * c + 128], T.x2[:, c, :]).then_inc(S.qx, 1)
    v.wait_ge(S.qwl, 16)
    v.quantize_mx(T.wc[:], T.ws[:], T.qwt[:]).then_inc(S.qq, 1)

    t.wait_ge(S.qh, 1)
    t.wait_ge(S.qx, 3)
    t.wait_ge(S.hpa, (N - 1) * 2 * neng)
    t.matmul_mx(T.acc[:, 0:X2], T.hpc[:, 8:136], T.hps[:, 8:136], T.xc[:], T.xs[:], True, True).then_inc(S.bm, 1)
    t.wait_ge(S.qq, 1)
    t.wait_ge(S.qe, 1)
    bank = {}
    for i, m in enumerate(units):
        for q in m:
            if q != rank:
                t.wait_ge(S["ea%d" % q], 2 * neng)
        w = slice(K * m[0], K * m[0] + K * len(m))
        for o in range(O):
            b = 1 + O * i + o
            if b == 8:
                t.wait_ge(S.cmp, 1)
            if b > 8:
                t.wait_ge(S.tco, O)
            b = b % 8
            bank[i, o] = 512 * b
            t.matmul_mx(T.acc[:, 512 * b:512 * b + K * len(m)], T.wc[:, 128 * o:128 * o + 128],
                        T.ws[:, 128 * o:128 * o + 128], T.ec[:, w], T.es[:, w], True, True).then_inc(S["tm%d" % o], 1)

    v.wait_ge(S.bm, 1)
    v.tensor_scalar(T.bits[0:PL, :], T.acc[0:PL, 0:X2], 0.0, 128.0, AluOpType.is_gt, AluOpType.mult).then_inc(S.cmp, 1)
    v.wait_ge(S.cmp, 1)
    v.transpose(T.turn[0:PL, :], T.bits[0:PL, :]).then_inc(S.trn, 1)
    v.wait_ge(S.trn, 1)
    v.wait_ge(S.halfm, 2)
    v.tensor_tensor_scan(T.scan[0:PL, :], T.half[0:PL, :], T.turn[0:PL, :], 0.0, AluOpType.mult, AluOpType.add
                         ).then_inc(S.scn, 1)
    v.wait_ge(S.scn, 1)
    for k in range(H):
        low = (rank % H) ^ k ^ (H - 1)
        v.tensor_copy(T.buck[0:PL, RUNS * low:RUNS * low + RUNS], T.scan[0:PL, NBIT * k + NBIT - 1:X2:NBIT * H]
                      ).then_inc(S.rord, 1)
    v.wait_ge(S.rord, H)
    half_of = (1 - rank // H, rank // H)
    for to in range(0, 128, 32):
        for s in range(2):
            h = HR * half_of[s]
            v.tensor_copy(T.offs[to:to + 32, h:h + HR], T.buck[32 * s:32 * s + 32, :]).then_inc(S.lst, 1)
    v.wait_ge(S.lst, 8)

    for i, m in enumerate(units):
        w = slice(K * m[0], K * m[0] + K * len(m))
        for o, eng in ((1, a), (0, v)):
            tab, tc = T["tab%d" % o], S["tc%d" % o]
            b = slice(bank[i, o], bank[i, o] + K * len(m))
            if i == 0:
                if o == 1:
                    for p in range(O):
                        a.wait_ge(S["tm%d" % p], 1)
                        a.activation(T["tab%d" % p][:, w], T.acc[:, bank[i, p]:bank[i, p] + K], Copy).then_inc(S.tco, 1)
                    a.wait_ge(S.lst, 8)
                eng.wait_ge(S.tco, O)
            else:
                eng.wait_ge(S["tm%d" % o], i + 1)
                if o == 0:
                    v.tensor_copy(tab[:, w], T.acc[:, b]).then_inc(tc, 1)
                else:
                    a.activation(tab[:, w], T.acc[:, b], Copy).then_inc(tc, 1)
                eng.wait_ge(tc, i)
            for q in m:
                k = (q * O + o) * TOK
                pick = tab[:, K * q:K * q + K].indirect(T.offs[:, RUNS * q:RUNS * q + RUNS])
                if o == 0:
                    v.tensor_copy(T.yb[:, k:k + TOK], pick).then_inc(S["yr%d" % q], 1)
                else:
                    a.activation(T.yb[:, k:k + TOK], pick, Copy).then_inc(S["yr%d" % q], 1)
        if i == 0:
            a.wait_ge(S.bkc, 1)
            for j in range(2):
                a.activation(T.bkp[0:PL, 32 * j:32 * j + 2 * RUNS], T.buck[0:PL, 2 * RUNS * j:2 * RUNS * j + 2 * RUNS],
                             Copy).then_inc(S.bkc, 1)
        if i == 1:
            v.wait_ge(S.bkc, 3)
            v.transpose(T.bkt[0:PL, :], T.bkp[0:PL, :]).then_inc(S.bkr, 1)

    nst = 0
    for i, u in enumerate(pairs):
        parts = [[2 * u], [2 * u + 1]] if i == len(pairs) - 1 else [[2 * u, 2 * u + 1]]
        for m in parts:
            for q in m:
                sy.wait_ge(S["yr%d" % q], O)
            w = slice(O * TOK * m[0], O * TOK * (m[0] + len(m)))
            sy.dma_start(T.y[:, w], T.yb[:, w]).then_inc(S.stored, 16)
            nst += 1
        if i == 0:
            sy.wait_ge(S.bkr, 1)
            for s in range(2):
                for j in range(2):
                    q = H * half_of[s] + 2 * j
                    sy.dma_start(T.bk[q:q + 2, :], T.bkt[32 * s:32 * s + 2 * RUNS, 32 * j:32 * j + 16]
                                 ).then_inc(S.stored, 16)
                    nst += 1
    sy.wait_ge(S.stored, 16 * nst)
